import numpy as np
import ml_dtypes


def mxq(x, axis, fmt="e4m3"):
    dtype, down = {"e4m3": (ml_dtypes.float8_e4m3fn, 7), "e5m2": (ml_dtypes.float8_e5m2, 14)}[fmt]
    v = np.moveaxis(np.asarray(x, np.float32).astype(ml_dtypes.bfloat16).astype(np.float64), axis, -1)
    blocks = v.reshape(v.shape[:-1] + (-1, 32))
    amax = np.abs(blocks).max(-1, keepdims=True)
    byte = np.maximum(np.where(amax > 0, np.frexp(amax)[1] - 1 + 127, 0) - down, 1)
    scale = np.exp2(byte - 127.0)
    codes = (blocks / scale).astype(np.float32).astype(dtype).astype(np.float64)
    return np.moveaxis((codes * scale).reshape(v.shape), -1, axis)


WIDE = False


def mx_kscale(k):
    if not WIDE:
        return np.ones(k)
    levels = np.array([10, -10, 5, -5, 0])
    if k % 512:
        return np.exp2(np.random.permutation(np.resize(levels, k // 32))).repeat(32)
    a = np.empty((k // 512, 16))
    for p in range(k // 512):
        a[p, :8] = np.random.permutation(np.resize(levels, 8))
        for g in range(8):
            far = levels[np.abs(levels - a[p, g]) >= 10]
            a[p, g + 8] = far[np.random.randint(len(far))]
    return np.exp2(a.ravel()).repeat(32)


def f64(x):
    return np.asarray(x).astype(np.float64)


def striped(idx):
    return np.tile(idx.reshape(-1, 16).T, (8, 1)).astype(np.uint16)


def unstriped(offs):
    return offs[:16].T.reshape(-1).astype(np.int64)


def pack_weight(w):
    k, n = w.shape
    w = f64(np.asarray(w, np.float32).astype(ml_dtypes.bfloat16)).reshape(k // 32, 32, n)
    amax = np.abs(w).max(1)
    byte = np.clip(np.where(amax > 0, np.frexp(amax)[1] - 1 + 127 - 7, 1), 1, 254)
    scaled = (w * np.exp2(127.0 - byte)[:, None, :]).reshape(k, n).astype(np.float32)
    words = np.ascontiguousarray(scaled.reshape(k // 512, 128, 4, n).transpose(0, 1, 3, 2)).astype(ml_dtypes.float8_e4m3fn).view(np.uint8)
    return words, np.ascontiguousarray(byte.astype(np.uint8).reshape(k // 512, 16, n))


def unpack_weight(words, scales):
    g, p, n, _ = words.shape
    vals = np.ascontiguousarray(words).view(ml_dtypes.float8_e4m3fn).astype(np.float64) * np.repeat(np.exp2(scales.astype(np.float64) - 127.0), 8, axis=1)[..., None]
    return vals.transpose(0, 1, 3, 2).reshape(g * 512, n)


E2M1 = np.array([0.0, 0.5, 1.0, 1.5, 2.0, 3.0, 4.0, 6.0, -0.0, -0.5, -1.0, -1.5, -2.0, -3.0, -4.0, -6.0])


def pack_fp4(w):
    k, n = w.shape
    w = f64(np.asarray(w, np.float32).astype(ml_dtypes.bfloat16)).reshape(k // 32, 32, n)
    amax = np.abs(w).max(1)
    mant, ex = np.frexp(amax / 6.0)
    byte = np.clip(np.where(amax > 0, np.where(mant > 0.5, ex, ex - 1) + 127, 1), 1, 254)
    scaled = (w * np.exp2(127.0 - byte)[:, None, :]).reshape(k, n).astype(np.float32)
    c = np.ascontiguousarray(scaled.reshape(k // 512, 128, 4, n).transpose(0, 1, 3, 2)).astype(ml_dtypes.float4_e2m1fn).view(np.uint8) & 0xF
    words = (c[..., 0::2] | (c[..., 1::2] << 4)).reshape(k // 512, 128, 2 * n)
    return np.ascontiguousarray(words), np.ascontiguousarray(byte.astype(np.uint8).reshape(k // 512, 16, n))


def unpack_fp4(words, scales):
    g, _, n = scales.shape
    words = np.ascontiguousarray(words).reshape(g, 128, n, 2)
    nib = np.empty((g, 128, n, 4), np.uint8)
    nib[..., 0::2] = words & 0xF
    nib[..., 1::2] = words >> 4
    vals = E2M1[nib] * np.repeat(np.exp2(scales.astype(np.float64) - 127.0), 8, axis=1)[..., None]
    return vals.transpose(0, 1, 3, 2).reshape(g * 512, n)


def sigmoid(v):
    return 1.0 / (1.0 + np.exp(-np.maximum(v, -700.0)))


K, T, S, D, H, Z, W = 512, 2048, 512, 2, 512, 512, 2048
P = 2 ** 7


def setup_inputs():
    n = np.random.standard_normal
    s = mx_kscale(K)[:, None]
    u = mx_kscale(H)
    packed_xT = pack_weight(n((K, T)) * s)
    packed_w1 = pack_fp4(n((K, H)) / np.sqrt(K) / s)
    packed_eT = pack_weight(n((K, W)) * s)
    packed_w2 = pack_fp4(n((K, H)) / np.sqrt(K) / s)
    packed_w3 = pack_fp4(n((K, H)) / np.sqrt(K) / s)
    return {
        "x_words": packed_xT[0],
        "x_scales": packed_xT[1],
        "w1_words": packed_w1[0],
        "w1_scales": packed_w1[1],
        "e_words": packed_eT[0],
        "e_scales": packed_eT[1],
        "w2_words": packed_w2[0],
        "w2_scales": packed_w2[1],
        "w3_words": packed_w3[0],
        "w3_scales": packed_w3[1],
        "unit": (np.random.uniform(0.6, 1.4, (H, 1)) * u[:, None]).astype(np.float32),
        "unit2": (np.random.uniform(0.6, 1.4, (H, 1)) / np.sqrt(H) / u[:, None]).astype(np.float32),
        "prc": (np.tile(np.random.uniform(0.1, 1.2, W), (P, 1))).astype(np.float32),
        "offs": striped(np.random.permutation(T)[:S]),
        "firm": striped(np.random.permutation(W)[:Z]),
        "ind": striped(np.random.permutation(Z)),
    }


def reference(x_words, x_scales, w1_words, w1_scales, e_words, e_scales, w2_words, w2_scales, w3_words, w3_scales, unit, unit2, prc, offs, firm, ind):
    xq = unpack_weight(x_words, x_scales)[:, unstriped(offs)]
    y = unpack_fp4(w1_words, w1_scales).T @ xq
    ny = -0.5 * y
    skl = np.maximum(y.reshape(len(y), -1, D).sum(axis=2), ny.reshape(len(ny), -1, D).sum(axis=2))
    hid = f64(unit) * skl
    e_firm = unpack_weight(e_words, e_scales)[:, unstriped(firm)]
    ye = unpack_fp4(w2_words, w2_scales).T @ e_firm
    yw = unpack_fp4(w3_words, w3_scales).T @ e_firm
    wi = yw[:, unstriped(ind)]
    ri = sigmoid(wi)
    fr = ye * ri
    hid2 = f64(unit2) * fr
    sc = mxq(hid, 0, "e4m3").T @ mxq(hid2, 0, "e4m3")
    net = sc - (f64(prc)[:1][:, unstriped(firm)])
    mu_ = np.exp(1.0 * np.tanh(net))
    marg = mu_.mean(axis=1, keepdims=True)
    half = mu_ / (np.sqrt(marg) + 0.2)
    return np.log(half + 0.3) * (f64(prc)[:1][:, unstriped(firm)])

@@ -1,0 +1,218 @@
+import math
+from contextlib import ExitStack
+
+import concourse.mybir as mybir
+
+K, T, S, H, Z, W = 512, 2048, 512, 512, 512, 2048
+V = S // 2
+FLOPS = 2 * K * H * (S + 2 * Z) + 2 * H * V * Z
+
+F32 = mybir.dt.float32
+BF16 = mybir.dt.bfloat16
+I32 = mybir.dt.int32
+U32 = mybir.dt.uint32
+U16 = mybir.dt.uint16
+U8 = mybir.dt.uint8
+FP8X4 = mybir.dt.float8_e4m3fn_x4
+FP4X4 = mybir.dt.float4_e2m1fn_x4
+ALU = mybir.AluOpType
+ACT = mybir.ActivationFunctionType
+
+P = 128
+SLOTS = 4
+HALF = Z // 2
+
+
+def tile_picked_ymatchm_log_p_kernel(
+    tc, x_words, x_scales, w1_words, w1_scales, e_words, e_scales, w2_words, w2_scales,
+    w3_words, w3_scales, unit, unit2, prc, offs, firm, ind, out,
+):
+    nc = tc.nc
+    with ExitStack() as ctx:
+        sb = ctx.enter_context(tc.tile_pool(name="sb", bufs=1))
+        ps = ctx.enter_context(tc.psum_pool(name="ps", bufs=1))
+
+        def tile(name, shape, dtype):
+            return sb.tile(shape, dtype, name=name, align_bytes=64)
+
+        def bank(name, index):
+            return ps.tile([P, 512], F32, name=name, tag="bank%d" % index)
+
+        def load_list(name, src):
+            dst = sb.tile([P, src.shape[1]], U16, name=name)
+            nc.sync.dma_start(dst[:], src)
+            return dst
+
+        def load_scales(name, src, zero_engine, queue):
+            dst = tile(name, [P, src.shape[2]], U8)
+            zero_engine.memset(dst[:].bitcast(I32), 0)
+            for quad in range(4):
+                queue.dma_start(dst[32 * quad : 32 * quad + 4, :].bitcast(I32), src[0, 4 * quad : 4 * quad + 4, :].bitcast(I32))
+            return dst
+
+        def load_table(name, src):
+            dst = tile(name, [P, src.shape[2]], I32)
+            nc.sync.dma_start(dst[:], src[0].rearrange("p n r -> p (n r)").bitcast(I32))
+            return dst
+
+        def load_weight(name, words, scales, zero_engine, queue):
+            raw = tile(name + "_raw", [P, 2 * H], U8)
+            nc.sync.dma_start(raw[:].bitcast(I32), words[0].bitcast(I32))
+            raw_scales = load_scales(name + "_raw_scales", scales, zero_engine, queue)
+            dealt = tile(name + "_codes", [P, 2 * H], U8)
+            dealt_scales = tile(name + "_scales", [P, H], U8)
+            for dst, src in ((dealt, raw), (dealt_scales, raw_scales)):
+                nc.scalar.copy(
+                    dst[:].bitcast(U32).rearrange("p (t g r) -> p t g r", t=SLOTS, g=16),
+                    src[:].bitcast(U32).rearrange("p (g t r) -> p t g r", t=SLOTS, g=16),
+                )
+            return dealt, dealt_scales
+
+        def weight_matmul(dst, weight, t, codes, scales, start, stop):
+            nc.tensor.matmul_mx(
+                out=dst,
+                lhsT=weight[0][:, 2 * P * t : 2 * P * (t + 1)].bitcast(FP4X4),
+                lhsT_scale=weight[1][:, P * t : P * (t + 1)],
+                rhs=codes.bitcast(FP8X4),
+                rhs_scale=scales,
+                start=start,
+                stop=stop,
+            )
+
+        e_table = load_table("e_table", e_words)
+        firm_sb = load_list("firm_sb", firm)
+        e_scale_table = load_scales("e_scale_table", e_scales, nc.gpsimd, nc.sync)
+        w3 = load_weight("w3", w3_words, w3_scales, nc.vector, nc.sync)
+        offs_sb = load_list("offs_sb", offs)
+        x_table = load_table("x_table", x_words)
+        x_scale_table = load_scales("x_scale_table", x_scales, nc.gpsimd, nc.sync)
+        ind_sb = load_list("ind_sb", ind)
+        w2 = load_weight("w2", w2_words, w2_scales, nc.gpsimd, nc.sync)
+
+        unit_rows = tile("unit_rows", [P, P], F32)
+        nc.gpsimd.memset(unit_rows[:], 0.0)
+        for row, src in ((0, unit), (1, unit2)):
+            nc.sync.dma_start(unit_rows[row:P:32, :], src.rearrange("(a n) o -> a (n o)", a=4))
+        w1 = load_weight("w1", w1_words, w1_scales, nc.gpsimd, nc.sync)
+        prc_table = tile("prc_table", [P, W], F32)
+        nc.sync.dma_start(prc_table[:], prc)
+
+        unit_sorted = tile("unit_sorted", [P, P], F32)
+        nc.vector.tensor_copy(
+            unit_sorted[:].rearrange("p (t g q) -> p t g q", t=SLOTS, q=8), unit_rows[:].rearrange("p (g t q) -> p t g q", t=SLOTS, q=8)
+        )
+        unit_cols = tile("unit_cols", [P, P], F32)
+        nc.vector.transpose(unit_cols[:], unit_sorted[:])
+        unit_abs = tile("unit_abs", [P, SLOTS], F32)
+        nc.scalar.activation(unit_abs[:], unit_cols[:, 0:P:32], ACT.Abs)
+        unit_step = tile("unit_step", [P, SLOTS], F32)
+        nc.vector.tensor_scalar(unit_step[:], unit_cols[:, 0:P:32], 0.0, 2.0, ALU.is_ge, ALU.mult)
+        unit2_signed = tile("unit2_signed", [P, SLOTS], F32)
+        nc.vector.scalar_tensor_tensor(unit2_signed[:], unit_step[:], -1.0, unit_cols[:, 1:P:32], ALU.add, ALU.mult)
+
+        e_sc = tile("e_sc", [P, Z], U8)
+        nc.vector.tensor_copy(e_sc[:], e_scale_table[:].indirect(firm_sb[:]))
+        e_codes = tile("e_codes", [P, Z], U32)
+        nc.vector.tensor_copy(e_codes[:], e_table[:].bitcast(U32).indirect(firm_sb[:]))
+
+        gate = []
+        for t in range(SLOTS):
+            yw = bank("yw%d" % t, t)
+            weight_matmul(yw[:], w3, t, e_codes[:], e_sc[:], True, True)
+            gate.append(tile("gate%d" % t, [P, Z], F32))
+            nc.scalar.activation(gate[t][:], yw[:], ACT.Tanh, scale=0.5)
+        ye = []
+        for t in range(SLOTS):
+            ye.append(bank("ye%d" % t, SLOTS + t))
+            weight_matmul(ye[t][:], w2, t, e_codes[:], e_sc[:], True, True)
+
+        x_sc = tile("x_sc", [P, S], U8)
+        nc.vector.tensor_copy(x_sc[:].rearrange("p (d v) -> p v d", d=2), x_scale_table[:].indirect(offs_sb[:]))
+        x_codes = tile("x_codes", [P, S], U32)
+        nc.vector.tensor_copy(x_codes[:].rearrange("p (d v) -> p v d", d=2), x_table[:].bitcast(U32).indirect(offs_sb[:]))
+
+        hid = []
+        for b in range(2):
+            pair_sum = bank("pair_sum%d" % b, b)
+            for t in range(SLOTS):
+                for d in range(2):
+                    cols = slice(V * d + P * b, V * d + P * (b + 1))
+                    weight_matmul(pair_sum[:, P * t : P * (t + 1)], w1, t, x_codes[:, cols], x_sc[:, cols], d == 0, d == 1)
+            scaled = tile("scaled%d" % b, [P, P * SLOTS], F32)
+            nc.vector.tensor_tensor(
+                scaled[:].rearrange("p (v t) -> p v t", t=SLOTS),
+                pair_sum[:].rearrange("p (t v) -> p v t", t=SLOTS),
+                unit_abs[:].unsqueeze(1).to_broadcast([P, P, SLOTS]),
+                ALU.mult,
+            )
+            hid_bf = tile("hid_bf%d" % b, [P, P * SLOTS], BF16)
+            nc.vector.scalar_tensor_tensor(hid_bf[:], scaled[:], -0.5, scaled[:], ALU.mult, ALU.max)
+            hid_codes = tile("hid_codes%d" % b, [P, P], U32)
+            hid_sc = tile("hid_sc%d" % b, [P, P], U8)
+            nc.vector.quantize_mx(out=hid_codes[:].bitcast(FP8X4), scales=hid_sc[:], in_=hid_bf[:])
+            hid.append((hid_codes, hid_sc))
+
+        fee = tile("fee", [P, Z], F32)
+        nc.vector.tensor_copy(fee[:], prc_table[:].indirect(firm_sb[:]))
+
+        mu = [tile("mu%d" % b, [P, Z], F32) for b in range(2)]
+        sums = tile("sums", [P, 4], F32)
+        for h in range(2):
+            cols = slice(HALF * h, HALF * (h + 1))
+            planes = tile("planes%d" % h, [P, SLOTS * HALF], BF16)
+            for t in range(SLOTS):
+                sig = tile("sig%d_%d" % (h, t), [P, HALF], F32)
+                nc.scalar.activation(sig[:], gate[t][:].indirect(ind_sb[:, 16 * h : 16 * (h + 1)]), ACT.Copy, scale=0.5, bias=0.5)
+                nc.vector.scalar_tensor_tensor(
+                    planes[:, HALF * t : HALF * (t + 1)], sig[:], unit2_signed[:, t : t + 1], ye[t][:, cols], ALU.mult, ALU.mult
+                )
+            hid2_bf = tile("hid2_bf%d" % h, [P, HALF * SLOTS], BF16)
+            nc.vector.tensor_copy(
+                hid2_bf[:].rearrange("p (e t) -> p e t", t=SLOTS), planes[:].rearrange("p (t e) -> p e t", t=SLOTS)
+            )
+            hid2_codes = tile("hid2_codes%d" % h, [P, HALF], U32)
+            hid2_sc = tile("hid2_sc%d" % h, [P, HALF], U8)
+            nc.vector.quantize_mx(out=hid2_codes[:].bitcast(FP8X4), scales=hid2_sc[:], in_=hid2_bf[:])
+
+            sc = bank("sc%d" % h, 2 + h)
+            for b in range(2):
+                nc.tensor.matmul_mx(
+                    out=sc[:, HALF * b : HALF * (b + 1)],
+                    lhsT=hid[b][0][:].bitcast(FP8X4),
+                    lhsT_scale=hid[b][1][:],
+                    rhs=hid2_codes[:].bitcast(FP8X4),
+                    rhs_scale=hid2_sc[:],
+                    start=True,
+                    stop=True,
+                )
+            net = tile("net%d" % h, [P, 2 * HALF], F32)
+            nc.vector.tensor_tensor(
+                net[:].rearrange("p (b e) -> p b e", b=2),
+                sc[:].rearrange("p (b e) -> p b e", b=2),
+                fee[:, cols].unsqueeze(1).to_broadcast([P, 2, HALF]),
+                ALU.subtract,
+            )
+            squashed = tile("squashed%d" % h, [P, 2 * HALF], F32)
+            nc.scalar.activation(squashed[:], net[:], ACT.Tanh)
+            for b in range(2):
+                nc.scalar.activation(
+                    mu[b][:, cols], squashed[:, HALF * b : HALF * (b + 1)], ACT.Exp, accum_out=sums[:, 2 * h + b : 2 * h + b + 1]
+                )
+
+        total = tile("total", [P, 2], F32)
+        nc.vector.tensor_tensor(total[:], sums[:, 0:2], sums[:, 2:4], ALU.add)
+        one_half = tile("one_half", [P, 2], F32)
+        nc.gpsimd.memset(one_half[:], 0.5)
+        root = tile("root", [P, 2], F32)
+        nc.gpsimd.tensor_tensor(root[:], total[:], one_half[:], ALU.pow)
+        denom = tile("denom", [P, 2], F32)
+        nc.vector.tensor_scalar(denom[:], root[:], 1.0 / math.sqrt(Z), 0.2, ALU.mult, ALU.add)
+        inv = tile("inv", [P, 2], F32)
+        nc.vector.reciprocal(inv[:], denom[:])
+
+        for b in range(2):
+            logs = tile("logs%d" % b, [P, Z], F32)
+            nc.scalar.activation(logs[:], mu[b][:], ACT.Ln, scale=inv[:, b : b + 1], bias=0.3)
+            result = tile("result%d" % b, [P, Z], F32)
+            nc.vector.tensor_tensor(result[:], logs[:], fee[:], ALU.mult)
+            nc.sync.dma_start(out[P * b : P * (b + 1), :], result[:])

@@ -21,6 +21,7 @@ ACT = mybir.ActivationFunctionType
 P = 128
 SLOTS = 4
 HALF = Z // 2
+CHUNKS = ((0, 256), (256, 384), (384, 512))
 
 
 def tile_picked_ymatchm_log_p_kernel(
@@ -32,8 +33,8 @@ def tile_picked_ymatchm_log_p_kernel(
         sb = ctx.enter_context(tc.tile_pool(name="sb", bufs=1))
         ps = ctx.enter_context(tc.psum_pool(name="ps", bufs=1))
 
-        def tile(name, shape, dtype):
-            return sb.tile(shape, dtype, name=name, align_bytes=64)
+        def tile(name, shape, dtype, tag=""):
+            return sb.tile(shape, dtype, name=name, tag=tag or name, align_bytes=64)
 
         def bank(name, index):
             return ps.tile([P, 512], F32, name=name, tag="bank%d" % index)
@@ -55,18 +56,18 @@ def tile_picked_ymatchm_log_p_kernel(
             nc.sync.dma_start(dst[:], src[0].rearrange("p n r -> p (n r)").bitcast(I32))
             return dst
 
-        def load_weight(name, words, scales, zero_engine, queue):
+        def load_codes(name, words):
             raw = tile(name + "_raw", [P, 2 * H], U8)
             nc.sync.dma_start(raw[:].bitcast(I32), words[0].bitcast(I32))
-            raw_scales = load_scales(name + "_raw_scales", scales, zero_engine, queue)
-            dealt = tile(name + "_codes", [P, 2 * H], U8)
-            dealt_scales = tile(name + "_scales", [P, H], U8)
-            for dst, src in ((dealt, raw), (dealt_scales, raw_scales)):
-                nc.scalar.copy(
-                    dst[:].bitcast(U32).rearrange("p (t g r) -> p t g r", t=SLOTS, g=16),
-                    src[:].bitcast(U32).rearrange("p (g t r) -> p t g r", t=SLOTS, g=16),
-                )
-            return dealt, dealt_scales
+            return raw
+
+        def deal(name, src, copy):
+            dst = tile(name, src.shape, U8)
+            copy(
+                dst[:].bitcast(U32).rearrange("p (t g r) -> p t g r", t=SLOTS, g=16),
+                src[:].bitcast(U32).rearrange("p (g t r) -> p t g r", t=SLOTS, g=16),
+            )
+            return dst
 
         def weight_matmul(dst, weight, t, codes, scales, start, stop):
             nc.tensor.matmul_mx(
@@ -79,36 +80,29 @@ def tile_picked_ymatchm_log_p_kernel(
                 stop=stop,
             )
 
-        e_table = load_table("e_table", e_words)
         firm_sb = load_list("firm_sb", firm)
+        w3_raw = load_codes("w3", w3_words)
         e_scale_table = load_scales("e_scale_table", e_scales, nc.gpsimd, nc.sync)
-        w3 = load_weight("w3", w3_words, w3_scales, nc.vector, nc.sync)
-        offs_sb = load_list("offs_sb", offs)
+        e_table = load_table("e_table", e_words)
+        w3_raw_scales = load_scales("w3_raw_scales", w3_scales, nc.gpsimd, nc.sync)
         x_table = load_table("x_table", x_words)
-        x_scale_table = load_scales("x_scale_table", x_scales, nc.gpsimd, nc.sync)
+        offs_sb = load_list("offs_sb", offs)
         ind_sb = load_list("ind_sb", ind)
-        w2 = load_weight("w2", w2_words, w2_scales, nc.gpsimd, nc.sync)
-
+        x_scale_table = load_scales("x_scale_table", x_scales, nc.vector, nc.gpsimd)
         unit_rows = tile("unit_rows", [P, P], F32)
-        nc.gpsimd.memset(unit_rows[:], 0.0)
+        nc.vector.memset(unit_rows[:], 0.0)
         for row, src in ((0, unit), (1, unit2)):
-            nc.sync.dma_start(unit_rows[row:P:32, :], src.rearrange("(a n) o -> a (n o)", a=4))
-        w1 = load_weight("w1", w1_words, w1_scales, nc.gpsimd, nc.sync)
+            nc.gpsimd.dma_start(unit_rows[row:P:32, :], src.rearrange("(a n) o -> a (n o)", a=4))
+        w1_raw = load_codes("w1", w1_words)
+        w1_raw_scales = load_scales("w1_raw_scales", w1_scales, nc.vector, nc.sync)
+        w2_raw = load_codes("w2", w2_words)
+        w2_raw_scales = load_scales("w2_raw_scales", w2_scales, nc.vector, nc.sync)
+        w3 = (deal("w3_codes", w3_raw, nc.scalar.copy), deal("w3_sc", w3_raw_scales, nc.scalar.copy))
+        w1 = (deal("w1_codes", w1_raw, nc.gpsimd.tensor_copy), deal("w1_sc", w1_raw_scales, nc.gpsimd.tensor_copy))
+        w2 = (deal("w2_codes", w2_raw, nc.gpsimd.tensor_copy), deal("w2_sc", w2_raw_scales, nc.gpsimd.tensor_copy))
         prc_table = tile("prc_table", [P, W], F32)
         nc.sync.dma_start(prc_table[:], prc)
 
-        unit_sorted = tile("unit_sorted", [P, P], F32)
-        nc.vector.tensor_copy(
-            unit_sorted[:].rearrange("p (t g q) -> p t g q", t=SLOTS, q=8), unit_rows[:].rearrange("p (g t q) -> p t g q", t=SLOTS, q=8)
-        )
-        unit_cols = tile("unit_cols", [P, P], F32)
-        nc.vector.transpose(unit_cols[:], unit_sorted[:])
-        unit_abs = tile("unit_abs", [P, SLOTS], F32)
-        nc.scalar.activation(unit_abs[:], unit_cols[:, 0:P:32], ACT.Abs)
-        unit_step = tile("unit_step", [P, SLOTS], F32)
-        nc.vector.tensor_scalar(unit_step[:], unit_cols[:, 0:P:32], 0.0, 2.0, ALU.is_ge, ALU.mult)
-        unit2_signed = tile("unit2_signed", [P, SLOTS], F32)
-        nc.vector.scalar_tensor_tensor(unit2_signed[:], unit_step[:], -1.0, unit_cols[:, 1:P:32], ALU.add, ALU.mult)
 
         e_sc = tile("e_sc", [P, Z], U8)
         nc.vector.tensor_copy(e_sc[:], e_scale_table[:].indirect(firm_sb[:]))
@@ -121,24 +115,32 @@ def tile_picked_ymatchm_log_p_kernel(
             weight_matmul(yw[:], w3, t, e_codes[:], e_sc[:], True, True)
             gate.append(tile("gate%d" % t, [P, Z], F32))
             nc.scalar.activation(gate[t][:], yw[:], ACT.Tanh, scale=0.5)
-        ye = []
-        for t in range(SLOTS):
-            ye.append(bank("ye%d" % t, SLOTS + t))
-            weight_matmul(ye[t][:], w2, t, e_codes[:], e_sc[:], True, True)
 
         x_sc = tile("x_sc", [P, S], U8)
         nc.vector.tensor_copy(x_sc[:].rearrange("p (d v) -> p v d", d=2), x_scale_table[:].indirect(offs_sb[:]))
         x_codes = tile("x_codes", [P, S], U32)
         nc.vector.tensor_copy(x_codes[:].rearrange("p (d v) -> p v d", d=2), x_table[:].bitcast(U32).indirect(offs_sb[:]))
 
-        hid = []
-        for b in range(2):
+        unit_sorted = tile("unit_sorted", [P, P], F32, tag="x_table")
+        nc.vector.tensor_copy(
+            unit_sorted[:].rearrange("p (t g q) -> p t g q", t=SLOTS, q=8), unit_rows[:].rearrange("p (g t q) -> p t g q", t=SLOTS, q=8)
+        )
+        unit_cols = tile("unit_cols", [P, P], F32)
+        nc.vector.transpose(unit_cols[:], unit_sorted[:])
+        unit_abs = tile("unit_abs", [P, SLOTS], F32)
+        nc.vector.scalar_tensor_tensor(unit_abs[:], unit_cols[:, 0:P:32], -1.0, unit_cols[:, 0:P:32], ALU.mult, ALU.max)
+        unit_step = tile("unit_step", [P, SLOTS], F32)
+        nc.vector.tensor_scalar(unit_step[:], unit_cols[:, 0:P:32], 0.0, 2.0, ALU.is_ge, ALU.mult)
+        unit2_signed = tile("unit2_signed", [P, SLOTS], F32)
+        nc.vector.scalar_tensor_tensor(unit2_signed[:], unit_step[:], -1.0, unit_cols[:, 1:P:32], ALU.add, ALU.mult)
+
+        def make_hid(b, scratch_tag):
             pair_sum = bank("pair_sum%d" % b, b)
             for t in range(SLOTS):
                 for d in range(2):
                     cols = slice(V * d + P * b, V * d + P * (b + 1))
                     weight_matmul(pair_sum[:, P * t : P * (t + 1)], w1, t, x_codes[:, cols], x_sc[:, cols], d == 0, d == 1)
-            scaled = tile("scaled%d" % b, [P, P * SLOTS], F32)
+            scaled = tile("scaled%d" % b, [P, P * SLOTS], F32, tag=scratch_tag)
             nc.vector.tensor_tensor(
                 scaled[:].rearrange("p (v t) -> p v t", t=SLOTS),
                 pair_sum[:].rearrange("p (t v) -> p v t", t=SLOTS),
@@ -150,34 +152,37 @@ def tile_picked_ymatchm_log_p_kernel(
             hid_codes = tile("hid_codes%d" % b, [P, P], U32)
             hid_sc = tile("hid_sc%d" % b, [P, P], U8)
             nc.vector.quantize_mx(out=hid_codes[:].bitcast(FP8X4), scales=hid_sc[:], in_=hid_bf[:])
-            hid.append((hid_codes, hid_sc))
+            return hid_codes, hid_sc
 
-        fee = tile("fee", [P, Z], F32)
-        nc.vector.tensor_copy(fee[:], prc_table[:].indirect(firm_sb[:]))
-
-        mu = [tile("mu%d" % b, [P, Z], F32) for b in range(2)]
-        sums = tile("sums", [P, 4], F32)
-        for h in range(2):
-            cols = slice(HALF * h, HALF * (h + 1))
-            planes = tile("planes%d" % h, [P, SLOTS * HALF], BF16)
+        def gate_products(c):
+            lo, hi = CHUNKS[c]
+            n = hi - lo
+            planes = tile("planes%d" % c, [P, SLOTS * n], BF16)
             for t in range(SLOTS):
-                sig = tile("sig%d_%d" % (h, t), [P, HALF], F32)
-                nc.scalar.activation(sig[:], gate[t][:].indirect(ind_sb[:, 16 * h : 16 * (h + 1)]), ACT.Copy, scale=0.5, bias=0.5)
+                sig = tile("sig%d_%d" % (c, t), [P, n], F32)
+                nc.scalar.activation(sig[:], gate[t][:].indirect(ind_sb[:, lo // 16 : hi // 16]), ACT.Copy, scale=0.5, bias=0.5)
                 nc.vector.scalar_tensor_tensor(
-                    planes[:, HALF * t : HALF * (t + 1)], sig[:], unit2_signed[:, t : t + 1], ye[t][:, cols], ALU.mult, ALU.mult
+                    planes[:, n * t : n * (t + 1)], sig[:], unit2_signed[:, t : t + 1], ye[t][:, lo:hi], ALU.mult, ALU.mult
                 )
-            hid2_bf = tile("hid2_bf%d" % h, [P, HALF * SLOTS], BF16)
+            return planes
+
+        def interleave(c, planes):
+            hid2_bf = tile("hid2_bf%d" % c, planes.shape, BF16)
             nc.vector.tensor_copy(
                 hid2_bf[:].rearrange("p (e t) -> p e t", t=SLOTS), planes[:].rearrange("p (t e) -> p e t", t=SLOTS)
             )
-            hid2_codes = tile("hid2_codes%d" % h, [P, HALF], U32)
-            hid2_sc = tile("hid2_sc%d" % h, [P, HALF], U8)
-            nc.vector.quantize_mx(out=hid2_codes[:].bitcast(FP8X4), scales=hid2_sc[:], in_=hid2_bf[:])
+            return hid2_bf
 
-            sc = bank("sc%d" % h, 2 + h)
+        def match(c, hid2_bf):
+            lo, hi = CHUNKS[c]
+            n = hi - lo
+            hid2_codes = tile("hid2_codes%d" % c, [P, n], U32)
+            hid2_sc = tile("hid2_sc%d" % c, [P, n], U8)
+            nc.vector.quantize_mx(out=hid2_codes[:].bitcast(FP8X4), scales=hid2_sc[:], in_=hid2_bf[:])
+            sc = bank("sc%d" % c, (2 + c) % SLOTS)
             for b in range(2):
                 nc.tensor.matmul_mx(
-                    out=sc[:, HALF * b : HALF * (b + 1)],
+                    out=sc[:, n * b : n * (b + 1)],
                     lhsT=hid[b][0][:].bitcast(FP8X4),
                     lhsT_scale=hid[b][1][:],
                     rhs=hid2_codes[:].bitcast(FP8X4),
@@ -185,34 +190,62 @@ def tile_picked_ymatchm_log_p_kernel(
                     start=True,
                     stop=True,
                 )
-            net = tile("net%d" % h, [P, 2 * HALF], F32)
+            return sc
+
+        def exponentials(c, sc):
+            lo, hi = CHUNKS[c]
+            n = hi - lo
+            net = tile("net%d" % c, [P, 2 * n], F32)
             nc.vector.tensor_tensor(
                 net[:].rearrange("p (b e) -> p b e", b=2),
-                sc[:].rearrange("p (b e) -> p b e", b=2),
-                fee[:, cols].unsqueeze(1).to_broadcast([P, 2, HALF]),
+                sc[:, 0 : 2 * n].rearrange("p (b e) -> p b e", b=2),
+                fee[:, lo:hi].unsqueeze(1).to_broadcast([P, 2, n]),
                 ALU.subtract,
             )
-            squashed = tile("squashed%d" % h, [P, 2 * HALF], F32)
+            squashed = tile("squashed%d" % c, [P, 2 * n], F32)
             nc.scalar.activation(squashed[:], net[:], ACT.Tanh)
             for b in range(2):
-                nc.scalar.activation(
-                    mu[b][:, cols], squashed[:, HALF * b : HALF * (b + 1)], ACT.Exp, accum_out=sums[:, 2 * h + b : 2 * h + b + 1]
-                )
+                nc.scalar.activation(mu[b][:, lo:hi], squashed[:, n * b : n * (b + 1)], ACT.Exp, accum_out=sums[:, b, c : c + 1])
+
+        mu = [tile("mu%d" % b, [P, Z], F32) for b in range(2)]
+        sums = tile("sums", [P, 2, len(CHUNKS)], F32)
+        hid = [make_hid(0, "scaled0")]
+        ye = []
+        for t in range(SLOTS):
+            ye.append(bank("ye%d" % t, SLOTS + t))
+            weight_matmul(ye[t][:], w2, t, e_codes[:], e_sc[:], True, True)
+        planes0 = gate_products(0)
+        hid2_bf0 = interleave(0, planes0)
+        hid.append(make_hid(1, "sig0_%d" % (SLOTS - 1)))
+        sc0 = match(0, hid2_bf0)
+        planes1 = gate_products(1)
+        hid2_bf1 = interleave(1, planes1)
+        planes2 = gate_products(2)
+        fee = tile("fee", [P, Z], F32)
+        nc.scalar.activation(fee[:], prc_table[:].indirect(firm_sb[:]), ACT.Copy)
+        sc1 = match(1, hid2_bf1)
+        exponentials(0, sc0)
+        hid2_bf2 = interleave(2, planes2)
+        exponentials(1, sc1)
+        sc2 = match(2, hid2_bf2)
+        exponentials(2, sc2)
 
         total = tile("total", [P, 2], F32)
-        nc.vector.tensor_tensor(total[:], sums[:, 0:2], sums[:, 2:4], ALU.add)
+        nc.vector.tensor_reduce(total[:], sums[:], mybir.AxisListType.X, ALU.add)
         one_half = tile("one_half", [P, 2], F32)
-        nc.gpsimd.memset(one_half[:], 0.5)
+        nc.vector.memset(one_half[:], 0.5)
         root = tile("root", [P, 2], F32)
         nc.gpsimd.tensor_tensor(root[:], total[:], one_half[:], ALU.pow)
-        denom = tile("denom", [P, 2], F32)
-        nc.vector.tensor_scalar(denom[:], root[:], 1.0 / math.sqrt(Z), 0.2, ALU.mult, ALU.add)
-        inv = tile("inv", [P, 2], F32)
-        nc.vector.reciprocal(inv[:], denom[:])
+        shift = tile("shift", [P, 2], F32)
+        nc.vector.tensor_scalar(shift[:], root[:], 0.3 / math.sqrt(Z), 0.3 * 0.2, ALU.mult, ALU.add)
+        log_denom = tile("log_denom", [P, 2], F32)
+        nc.scalar.activation(log_denom[:], root[:], ACT.Ln, scale=1.0 / math.sqrt(Z), bias=0.2)
 
         for b in range(2):
-            logs = tile("logs%d" % b, [P, Z], F32)
-            nc.scalar.activation(logs[:], mu[b][:], ACT.Ln, scale=inv[:, b : b + 1], bias=0.3)
-            result = tile("result%d" % b, [P, Z], F32)
-            nc.vector.tensor_tensor(result[:], logs[:], fee[:], ALU.mult)
-            nc.sync.dma_start(out[P * b : P * (b + 1), :], result[:])
+            for h in range(2):
+                cols = slice(HALF * h, HALF * (h + 1))
+                logs = tile("logs%d_%d" % (b, h), [P, HALF], F32)
+                nc.scalar.activation(logs[:], mu[b][:, cols], ACT.Ln, bias=shift[:, b : b + 1])
+                result = tile("result%d_%d" % (b, h), [P, HALF], F32)
+                nc.vector.scalar_tensor_tensor(result[:], logs[:], log_denom[:, b : b + 1], fee[:, cols], ALU.subtract, ALU.mult)
+                nc.sync.dma_start(out[P * b : P * (b + 1), cols], result[:])

@@ -84,15 +84,21 @@ def tile_picked_ymatchm_log_p_kernel(
         w3_raw = load_codes("w3", w3_words)
         e_scale_table = load_scales("e_scale_table", e_scales, nc.gpsimd, nc.sync)
         e_table = load_table("e_table", e_words)
-        w3_raw_scales = load_scales("w3_raw_scales", w3_scales, nc.gpsimd, nc.sync)
-        x_table = load_table("x_table", x_words)
-        offs_sb = load_list("offs_sb", offs)
-        ind_sb = load_list("ind_sb", ind)
         x_scale_table = load_scales("x_scale_table", x_scales, nc.vector, nc.gpsimd)
+        prc_table = tile("prc_table", [P, W], F32)
+        nc.vector.memset(prc_table[:], 0.0)
+        nc.sync.dma_start(prc_table[0:1, :], prc[0:1, :])
+        w3_raw_scales = load_scales("w3_raw_scales", w3_scales, nc.gpsimd, nc.sync)
+        offs_sb = load_list("offs_sb", offs)
+        x_table = load_table("x_table", x_words)
+        ind_sb = load_list("ind_sb", ind)
         unit_rows = tile("unit_rows", [P, P], F32)
         nc.vector.memset(unit_rows[:], 0.0)
-        for row, src in ((0, unit), (1, unit2)):
-            nc.gpsimd.dma_start(unit_rows[row:P:32, :], src.rearrange("(a n) o -> a (n o)", a=4))
+        for row, src in ((0, unit), (SLOTS, unit2)):
+            nc.gpsimd.dma_start(
+                unit_rows[row : row + SLOTS, :].rearrange("t (g q) -> t g q", q=8),
+                src.rearrange("(g t q) o -> t g (q o)", t=SLOTS, q=8),
+            )
         w1_raw = load_codes("w1", w1_words)
         w1_raw_scales = load_scales("w1_raw_scales", w1_scales, nc.vector, nc.sync)
         w2_raw = load_codes("w2", w2_words)
@@ -100,8 +106,20 @@ def tile_picked_ymatchm_log_p_kernel(
         w3 = (deal("w3_codes", w3_raw, nc.scalar.copy), deal("w3_sc", w3_raw_scales, nc.scalar.copy))
         w1 = (deal("w1_codes", w1_raw, nc.gpsimd.tensor_copy), deal("w1_sc", w1_raw_scales, nc.gpsimd.tensor_copy))
         w2 = (deal("w2_codes", w2_raw, nc.gpsimd.tensor_copy), deal("w2_sc", w2_raw_scales, nc.gpsimd.tensor_copy))
-        prc_table = tile("prc_table", [P, W], F32)
-        nc.sync.dma_start(prc_table[:], prc)
+
+        ones = tile("ones", [P, P], F32)
+        nc.vector.memset(ones[:], 1.0)
+        count = tile("count", [P, P], F32)
+        nc.vector.tensor_tensor_scan(count[:], ones[:], ones[:], 0.0, ALU.mult, ALU.add)
+        lane = tile("lane", [P, 32], F32)
+        nc.vector.transpose(lane[:], count[:, 0:32])
+        identity = tile("identity", [P, P], F32)
+        for quad in range(4):
+            rows = slice(32 * quad, 32 * (quad + 1))
+            nc.vector.tensor_scalar(identity[rows, :], count[rows, :], 32.0 * quad, lane[rows, 0:1], ALU.subtract, ALU.is_equal)
+
+        fee_row = tile("fee_row", [P, Z], F32)
+        nc.scalar.activation(fee_row[:], prc_table[:].indirect(firm_sb[:]), ACT.Copy)
 
 
         e_sc = tile("e_sc", [P, Z], U8)
@@ -121,21 +139,28 @@ def tile_picked_ymatchm_log_p_kernel(
         x_codes = tile("x_codes", [P, S], U32)
         nc.vector.tensor_copy(x_codes[:].rearrange("p (d v) -> p v d", d=2), x_table[:].bitcast(U32).indirect(offs_sb[:]))
 
-        unit_sorted = tile("unit_sorted", [P, P], F32, tag="x_table")
-        nc.vector.tensor_copy(
-            unit_sorted[:].rearrange("p (t g q) -> p t g q", t=SLOTS, q=8), unit_rows[:].rearrange("p (g t q) -> p t g q", t=SLOTS, q=8)
-        )
-        unit_cols = tile("unit_cols", [P, P], F32)
-        nc.vector.transpose(unit_cols[:], unit_sorted[:])
-        unit_abs = tile("unit_abs", [P, SLOTS], F32)
-        nc.vector.scalar_tensor_tensor(unit_abs[:], unit_cols[:, 0:P:32], -1.0, unit_cols[:, 0:P:32], ALU.mult, ALU.max)
-        unit_step = tile("unit_step", [P, SLOTS], F32)
-        nc.vector.tensor_scalar(unit_step[:], unit_cols[:, 0:P:32], 0.0, 2.0, ALU.is_ge, ALU.mult)
-        unit2_signed = tile("unit2_signed", [P, SLOTS], F32)
-        nc.vector.scalar_tensor_tensor(unit2_signed[:], unit_step[:], -1.0, unit_cols[:, 1:P:32], ALU.add, ALU.mult)
+        fee_turned = bank("fee_turned", 0)
+        for j in range(Z // P):
+            nc.tensor.transpose(fee_turned[:, P * j : P * (j + 1)], fee_row[:, P * j : P * (j + 1)], identity[:])
+        fee_cols = tile("fee_cols", [P, Z // P], F32)
+        nc.scalar.copy(fee_cols[:], fee_turned[:, 0:Z:P])
 
-        def make_hid(b, scratch_tag):
-            pair_sum = bank("pair_sum%d" % b, b)
+        unit_cols = bank("unit_cols", 1)
+        nc.tensor.transpose(unit_cols[:, 0:P], unit_rows[:], identity[:])
+        unit_step = tile("unit_step", [P, SLOTS], F32, tag="x_table")
+        nc.vector.tensor_scalar(unit_step[:], unit_cols[:, 0:SLOTS], 0.0, 2.0, ALU.is_ge, ALU.mult)
+        signed = tile("signed", [P, 2, SLOTS], F32)
+        nc.vector.scalar_tensor_tensor(
+            signed[:],
+            unit_step[:].unsqueeze(1).to_broadcast([P, 2, SLOTS]),
+            -1.0,
+            unit_cols[:, 0 : 2 * SLOTS].rearrange("p (a t) -> p a t", a=2),
+            ALU.add,
+            ALU.mult,
+        )
+
+        def scale_pairs(b, scratch_tag):
+            pair_sum = bank("pair_sum%d" % b, 2 + b)
             for t in range(SLOTS):
                 for d in range(2):
                     cols = slice(V * d + P * b, V * d + P * (b + 1))
@@ -144,15 +169,19 @@ def tile_picked_ymatchm_log_p_kernel(
             nc.vector.tensor_tensor(
                 scaled[:].rearrange("p (v t) -> p v t", t=SLOTS),
                 pair_sum[:].rearrange("p (t v) -> p v t", t=SLOTS),
-                unit_abs[:].unsqueeze(1).to_broadcast([P, P, SLOTS]),
+                signed[:, 0:1, :].to_broadcast([P, P, SLOTS]),
                 ALU.mult,
             )
+            return scaled
+
+        def round_hid(b, scaled):
             hid_bf = tile("hid_bf%d" % b, [P, P * SLOTS], BF16)
             nc.vector.scalar_tensor_tensor(hid_bf[:], scaled[:], -0.5, scaled[:], ALU.mult, ALU.max)
-            hid_codes = tile("hid_codes%d" % b, [P, P], U32)
-            hid_sc = tile("hid_sc%d" % b, [P, P], U8)
-            nc.vector.quantize_mx(out=hid_codes[:].bitcast(FP8X4), scales=hid_sc[:], in_=hid_bf[:])
-            return hid_codes, hid_sc
+            return hid_bf
+
+        def quantize_hid(b, hid_bf):
+            cols = slice(P * b, P * (b + 1))
+            nc.vector.quantize_mx(out=hid_codes[:, cols].bitcast(FP8X4), scales=hid_sc[:, cols], in_=hid_bf[:])
 
         def gate_products(c):
             lo, hi = CHUNKS[c]
@@ -162,7 +191,7 @@ def tile_picked_ymatchm_log_p_kernel(
                 sig = tile("sig%d_%d" % (c, t), [P, n], F32)
                 nc.scalar.activation(sig[:], gate[t][:].indirect(ind_sb[:, lo // 16 : hi // 16]), ACT.Copy, scale=0.5, bias=0.5)
                 nc.vector.scalar_tensor_tensor(
-                    planes[:, n * t : n * (t + 1)], sig[:], unit2_signed[:, t : t + 1], ye[t][:, lo:hi], ALU.mult, ALU.mult
+                    planes[:, n * t : n * (t + 1)], sig[:], signed[:, 1, t : t + 1], ye[t][:, lo:hi], ALU.mult, ALU.mult
                 )
             return planes
 
@@ -179,56 +208,51 @@ def tile_picked_ymatchm_log_p_kernel(
             hid2_codes = tile("hid2_codes%d" % c, [P, n], U32)
             hid2_sc = tile("hid2_sc%d" % c, [P, n], U8)
             nc.vector.quantize_mx(out=hid2_codes[:].bitcast(FP8X4), scales=hid2_sc[:], in_=hid2_bf[:])
-            sc = bank("sc%d" % c, (2 + c) % SLOTS)
-            for b in range(2):
+            turned = bank("turned%d" % c, c % 2)
+            for j in range(n // P):
+                block = lo // P + j
+                cols = slice(P * j, P * (j + 1))
+                sc = bank("sc%d" % block, 2 + block % 2)
                 nc.tensor.matmul_mx(
-                    out=sc[:, n * b : n * (b + 1)],
-                    lhsT=hid[b][0][:].bitcast(FP8X4),
-                    lhsT_scale=hid[b][1][:],
-                    rhs=hid2_codes[:].bitcast(FP8X4),
-                    rhs_scale=hid2_sc[:],
+                    out=sc[:, 0:V],
+                    lhsT=hid2_codes[:, cols].bitcast(FP8X4),
+                    lhsT_scale=hid2_sc[:, cols],
+                    rhs=hid_codes[:].bitcast(FP8X4),
+                    rhs_scale=hid_sc[:],
                     start=True,
                     stop=True,
                 )
-            return sc
-
-        def exponentials(c, sc):
-            lo, hi = CHUNKS[c]
-            n = hi - lo
-            net = tile("net%d" % c, [P, 2 * n], F32)
-            nc.vector.tensor_tensor(
-                net[:].rearrange("p (b e) -> p b e", b=2),
-                sc[:, 0 : 2 * n].rearrange("p (b e) -> p b e", b=2),
-                fee[:, lo:hi].unsqueeze(1).to_broadcast([P, 2, n]),
-                ALU.subtract,
-            )
-            squashed = tile("squashed%d" % c, [P, 2 * n], F32)
-            nc.scalar.activation(squashed[:], net[:], ACT.Tanh)
+                squashed = tile("squashed%d" % block, [P, V], F32)
+                nc.scalar.activation(squashed[:], sc[:, 0:V], ACT.Tanh, scale=-1.0, bias=fee_cols[:, block : block + 1])
+                for b in range(2):
+                    nc.tensor.transpose(turned[:, n * b + P * j : n * b + P * (j + 1)], squashed[:, P * b : P * (b + 1)], identity[:])
             for b in range(2):
-                nc.scalar.activation(mu[b][:, lo:hi], squashed[:, n * b : n * (b + 1)], ACT.Exp, accum_out=sums[:, b, c : c + 1])
+                nc.scalar.activation(mu[b][:, lo:hi], turned[:, n * b : n * (b + 1)], ACT.Exp, scale=-1.0, accum_out=sums[:, b, c : c + 1])
 
         mu = [tile("mu%d" % b, [P, Z], F32) for b in range(2)]
         sums = tile("sums", [P, 2, len(CHUNKS)], F32)
-        hid = [make_hid(0, "scaled0")]
+        hid_codes = tile("hid_codes", [P, V], U32)
+        hid_sc = tile("hid_sc", [P, V], U8)
+        quantize_hid(0, round_hid(0, scale_pairs(0, "scaled0")))
         ye = []
         for t in range(SLOTS):
             ye.append(bank("ye%d" % t, SLOTS + t))
             weight_matmul(ye[t][:], w2, t, e_codes[:], e_sc[:], True, True)
         planes0 = gate_products(0)
+        scaled1 = scale_pairs(1, "sig0_%d" % (SLOTS - 2))
         hid2_bf0 = interleave(0, planes0)
-        hid.append(make_hid(1, "sig0_%d" % (SLOTS - 1)))
-        sc0 = match(0, hid2_bf0)
+        quantize_hid(1, round_hid(1, scaled1))
+        match(0, hid2_bf0)
         planes1 = gate_products(1)
         hid2_bf1 = interleave(1, planes1)
         planes2 = gate_products(2)
-        fee = tile("fee", [P, Z], F32)
-        nc.scalar.activation(fee[:], prc_table[:].indirect(firm_sb[:]), ACT.Copy)
-        sc1 = match(1, hid2_bf1)
-        exponentials(0, sc0)
+        match(1, hid2_bf1)
         hid2_bf2 = interleave(2, planes2)
-        exponentials(1, sc1)
-        sc2 = match(2, hid2_bf2)
-        exponentials(2, sc2)
+        match(2, hid2_bf2)
+
+        fee = bank("fee", SLOTS)
+        for j in range(Z // P):
+            nc.tensor.transpose(fee[:, P * j : P * (j + 1)], fee_cols[:, j : j + 1].to_broadcast([P, P]), identity[:])
 
         total = tile("total", [P, 2], F32)
         nc.vector.tensor_reduce(total[:], sums[:], mybir.AxisListType.X, ALU.add)

import math
from contextlib import ExitStack

import concourse.mybir as mybir

K, T, S, H, Z, W = 512, 2048, 512, 512, 512, 2048
V = S // 2
FLOPS = 2 * K * H * (S + 2 * Z) + 2 * H * V * Z

F32 = mybir.dt.float32
BF16 = mybir.dt.bfloat16
I32 = mybir.dt.int32
U32 = mybir.dt.uint32
U16 = mybir.dt.uint16
U8 = mybir.dt.uint8
FP8X4 = mybir.dt.float8_e4m3fn_x4
FP4X4 = mybir.dt.float4_e2m1fn_x4
ALU = mybir.AluOpType
ACT = mybir.ActivationFunctionType

P = 128
SLOTS = 4
HALF = Z // 2
CHUNKS = ((0, 256), (256, 384), (384, 512))


def tile_picked_ymatchm_log_p_kernel(
    tc, x_words, x_scales, w1_words, w1_scales, e_words, e_scales, w2_words, w2_scales,
    w3_words, w3_scales, unit, unit2, prc, offs, firm, ind, out,
):
    nc = tc.nc
    with ExitStack() as ctx:
        sb = ctx.enter_context(tc.tile_pool(name="sb", bufs=1))
        ps = ctx.enter_context(tc.psum_pool(name="ps", bufs=1))

        def tile(name, shape, dtype, tag=""):
            return sb.tile(shape, dtype, name=name, tag=tag or name, align_bytes=64)

        def bank(name, index):
            return ps.tile([P, 512], F32, name=name, tag="bank%d" % index)

        def load_list(name, src):
            dst = sb.tile([P, src.shape[1]], U16, name=name)
            nc.sync.dma_start(dst[:], src)
            return dst

        def load_scales(name, src, zero_engine, queue):
            dst = tile(name, [P, src.shape[2]], U8)
            zero_engine.memset(dst[:].bitcast(I32), 0)
            for quad in range(4):
                queue.dma_start(dst[32 * quad : 32 * quad + 4, :].bitcast(I32), src[0, 4 * quad : 4 * quad + 4, :].bitcast(I32))
            return dst

        def load_table(name, src):
            dst = tile(name, [P, src.shape[2]], I32)
            nc.sync.dma_start(dst[:], src[0].rearrange("p n r -> p (n r)").bitcast(I32))
            return dst

        def load_codes(name, words):
            raw = tile(name + "_raw", [P, 2 * H], U8)
            nc.sync.dma_start(raw[:].bitcast(I32), words[0].bitcast(I32))
            return raw

        def deal(name, src, copy):
            dst = tile(name, src.shape, U8)
            copy(
                dst[:].bitcast(U32).rearrange("p (t g r) -> p t g r", t=SLOTS, g=16),
                src[:].bitcast(U32).rearrange("p (g t r) -> p t g r", t=SLOTS, g=16),
            )
            return dst

        def weight_matmul(dst, weight, t, codes, scales, start, stop):
            nc.tensor.matmul_mx(
                out=dst,
                lhsT=weight[0][:, 2 * P * t : 2 * P * (t + 1)].bitcast(FP4X4),
                lhsT_scale=weight[1][:, P * t : P * (t + 1)],
                rhs=codes.bitcast(FP8X4),
                rhs_scale=scales,
                start=start,
                stop=stop,
            )

        firm_sb = load_list("firm_sb", firm)
        w3_raw = load_codes("w3", w3_words)
        e_scale_table = load_scales("e_scale_table", e_scales, nc.gpsimd, nc.sync)
        e_table = load_table("e_table", e_words)
        x_scale_table = load_scales("x_scale_table", x_scales, nc.vector, nc.gpsimd)
        prc_table = tile("prc_table", [P, W], F32)
        nc.vector.memset(prc_table[:], 0.0)
        nc.sync.dma_start(prc_table[0:1, :], prc[0:1, :])
        w3_raw_scales = load_scales("w3_raw_scales", w3_scales, nc.gpsimd, nc.sync)
        offs_sb = load_list("offs_sb", offs)
        x_table = load_table("x_table", x_words)
        ind_sb = load_list("ind_sb", ind)
        unit_rows = tile("unit_rows", [P, P], F32)
        nc.vector.memset(unit_rows[:], 0.0)
        for row, src in ((0, unit), (SLOTS, unit2)):
            nc.gpsimd.dma_start(
                unit_rows[row : row + SLOTS, :].rearrange("t (g q) -> t g q", q=8),
                src.rearrange("(g t q) o -> t g (q o)", t=SLOTS, q=8),
            )
        w1_raw = load_codes("w1", w1_words)
        w1_raw_scales = load_scales("w1_raw_scales", w1_scales, nc.vector, nc.sync)
        w2_raw = load_codes("w2", w2_words)
        w2_raw_scales = load_scales("w2_raw_scales", w2_scales, nc.vector, nc.sync)
        w3 = (deal("w3_codes", w3_raw, nc.scalar.copy), deal("w3_sc", w3_raw_scales, nc.scalar.copy))
        w1 = (deal("w1_codes", w1_raw, nc.gpsimd.tensor_copy), deal("w1_sc", w1_raw_scales, nc.gpsimd.tensor_copy))
        w2 = (deal("w2_codes", w2_raw, nc.gpsimd.tensor_copy), deal("w2_sc", w2_raw_scales, nc.gpsimd.tensor_copy))

        ones = tile("ones", [P, P], F32)
        nc.vector.memset(ones[:], 1.0)
        count = tile("count", [P, P], F32)
        nc.vector.tensor_tensor_scan(count[:], ones[:], ones[:], 0.0, ALU.mult, ALU.add)
        lane = tile("lane", [P, 32], F32)
        nc.vector.transpose(lane[:], count[:, 0:32])
        identity = tile("identity", [P, P], F32)
        for quad in range(4):
            rows = slice(32 * quad, 32 * (quad + 1))
            nc.vector.tensor_scalar(identity[rows, :], count[rows, :], 32.0 * quad, lane[rows, 0:1], ALU.subtract, ALU.is_equal)

        fee_row = tile("fee_row", [P, Z], F32)
        nc.scalar.activation(fee_row[:], prc_table[:].indirect(firm_sb[:]), ACT.Copy)


        e_sc = tile("e_sc", [P, Z], U8)
        nc.vector.tensor_copy(e_sc[:], e_scale_table[:].indirect(firm_sb[:]))
        e_codes = tile("e_codes", [P, Z], U32)
        nc.vector.tensor_copy(e_codes[:], e_table[:].bitcast(U32).indirect(firm_sb[:]))

        gate = []
        for t in range(SLOTS):
            yw = bank("yw%d" % t, t)
            weight_matmul(yw[:], w3, t, e_codes[:], e_sc[:], True, True)
            gate.append(tile("gate%d" % t, [P, Z], F32))
            nc.scalar.activation(gate[t][:], yw[:], ACT.Tanh, scale=0.5)

        x_sc = tile("x_sc", [P, S], U8)
        nc.vector.tensor_copy(x_sc[:].rearrange("p (d v) -> p v d", d=2), x_scale_table[:].indirect(offs_sb[:]))
        x_codes = tile("x_codes", [P, S], U32)
        nc.vector.tensor_copy(x_codes[:].rearrange("p (d v) -> p v d", d=2), x_table[:].bitcast(U32).indirect(offs_sb[:]))

        fee_turned = bank("fee_turned", 0)
        for j in range(Z // P):
            nc.tensor.transpose(fee_turned[:, P * j : P * (j + 1)], fee_row[:, P * j : P * (j + 1)], identity[:])
        fee_cols = tile("fee_cols", [P, Z // P], F32)
        nc.scalar.copy(fee_cols[:], fee_turned[:, 0:Z:P])

        unit_cols = bank("unit_cols", 1)
        nc.tensor.transpose(unit_cols[:, 0:P], unit_rows[:], identity[:])
        unit_step = tile("unit_step", [P, SLOTS], F32, tag="x_table")
        nc.vector.tensor_scalar(unit_step[:], unit_cols[:, 0:SLOTS], 0.0, 2.0, ALU.is_ge, ALU.mult)
        signed = tile("signed", [P, 2, SLOTS], F32)
        nc.vector.scalar_tensor_tensor(
            signed[:],
            unit_step[:].unsqueeze(1).to_broadcast([P, 2, SLOTS]),
            -1.0,
            unit_cols[:, 0 : 2 * SLOTS].rearrange("p (a t) -> p a t", a=2),
            ALU.add,
            ALU.mult,
        )

        def scale_pairs(b, scratch_tag):
            pair_sum = bank("pair_sum%d" % b, 2 + b)
            for t in range(SLOTS):
                for d in range(2):
                    cols = slice(V * d + P * b, V * d + P * (b + 1))
                    weight_matmul(pair_sum[:, P * t : P * (t + 1)], w1, t, x_codes[:, cols], x_sc[:, cols], d == 0, d == 1)
            scaled = tile("scaled%d" % b, [P, P * SLOTS], F32, tag=scratch_tag)
            nc.vector.tensor_tensor(
                scaled[:].rearrange("p (v t) -> p v t", t=SLOTS),
                pair_sum[:].rearrange("p (t v) -> p v t", t=SLOTS),
                signed[:, 0:1, :].to_broadcast([P, P, SLOTS]),
                ALU.mult,
            )
            return scaled

        def round_hid(b, scaled):
            hid_bf = tile("hid_bf%d" % b, [P, P * SLOTS], BF16)
            nc.vector.scalar_tensor_tensor(hid_bf[:], scaled[:], -0.5, scaled[:], ALU.mult, ALU.max)
            return hid_bf

        def quantize_hid(b, hid_bf):
            cols = slice(P * b, P * (b + 1))
            nc.vector.quantize_mx(out=hid_codes[:, cols].bitcast(FP8X4), scales=hid_sc[:, cols], in_=hid_bf[:])

        def gate_products(c):
            lo, hi = CHUNKS[c]
            n = hi - lo
            planes = tile("planes%d" % c, [P, SLOTS * n], BF16)
            for t in range(SLOTS):
                sig = tile("sig%d_%d" % (c, t), [P, n], F32)
                nc.scalar.activation(sig[:], gate[t][:].indirect(ind_sb[:, lo // 16 : hi // 16]), ACT.Copy, scale=0.5, bias=0.5)
                nc.vector.scalar_tensor_tensor(
                    planes[:, n * t : n * (t + 1)], sig[:], signed[:, 1, t : t + 1], ye[t][:, lo:hi], ALU.mult, ALU.mult
                )
            return planes

        def interleave(c, planes):
            hid2_bf = tile("hid2_bf%d" % c, planes.shape, BF16)
            nc.vector.tensor_copy(
                hid2_bf[:].rearrange("p (e t) -> p e t", t=SLOTS), planes[:].rearrange("p (t e) -> p e t", t=SLOTS)
            )
            return hid2_bf

        def match(c, hid2_bf):
            lo, hi = CHUNKS[c]
            n = hi - lo
            hid2_codes = tile("hid2_codes%d" % c, [P, n], U32)
            hid2_sc = tile("hid2_sc%d" % c, [P, n], U8)
            nc.vector.quantize_mx(out=hid2_codes[:].bitcast(FP8X4), scales=hid2_sc[:], in_=hid2_bf[:])
            turned = bank("turned%d" % c, c % 2)
            for j in range(n // P):
                block = lo // P + j
                cols = slice(P * j, P * (j + 1))
                sc = bank("sc%d" % block, 2 + block % 2)
                nc.tensor.matmul_mx(
                    out=sc[:, 0:V],
                    lhsT=hid2_codes[:, cols].bitcast(FP8X4),
                    lhsT_scale=hid2_sc[:, cols],
                    rhs=hid_codes[:].bitcast(FP8X4),
                    rhs_scale=hid_sc[:],
                    start=True,
                    stop=True,
                )
                squashed = tile("squashed%d" % block, [P, V], F32)
                nc.scalar.activation(squashed[:], sc[:, 0:V], ACT.Tanh, scale=-1.0, bias=fee_cols[:, block : block + 1])
                for b in range(2):
                    nc.tensor.transpose(turned[:, n * b + P * j : n * b + P * (j + 1)], squashed[:, P * b : P * (b + 1)], identity[:])
            for b in range(2):
                nc.scalar.activation(mu[b][:, lo:hi], turned[:, n * b : n * (b + 1)], ACT.Exp, scale=-1.0, accum_out=sums[:, b, c : c + 1])

        mu = [tile("mu%d" % b, [P, Z], F32) for b in range(2)]
        sums = tile("sums", [P, 2, len(CHUNKS)], F32)
        hid_codes = tile("hid_codes", [P, V], U32)
        hid_sc = tile("hid_sc", [P, V], U8)
        quantize_hid(0, round_hid(0, scale_pairs(0, "scaled0")))
        ye = []
        for t in range(SLOTS):
            ye.append(bank("ye%d" % t, SLOTS + t))
            weight_matmul(ye[t][:], w2, t, e_codes[:], e_sc[:], True, True)
        planes0 = gate_products(0)
        scaled1 = scale_pairs(1, "sig0_%d" % (SLOTS - 2))
        hid2_bf0 = interleave(0, planes0)
        quantize_hid(1, round_hid(1, scaled1))
        match(0, hid2_bf0)
        planes1 = gate_products(1)
        hid2_bf1 = interleave(1, planes1)
        planes2 = gate_products(2)
        match(1, hid2_bf1)
        hid2_bf2 = interleave(2, planes2)
        match(2, hid2_bf2)

        fee = bank("fee", SLOTS)
        for j in range(Z // P):
            nc.tensor.transpose(fee[:, P * j : P * (j + 1)], fee_cols[:, j : j + 1].to_broadcast([P, P]), identity[:])

        total = tile("total", [P, 2], F32)
        nc.vector.tensor_reduce(total[:], sums[:], mybir.AxisListType.X, ALU.add)
        one_half = tile("one_half", [P, 2], F32)
        nc.vector.memset(one_half[:], 0.5)
        root = tile("root", [P, 2], F32)
        nc.gpsimd.tensor_tensor(root[:], total[:], one_half[:], ALU.pow)
        shift = tile("shift", [P, 2], F32)
        nc.vector.tensor_scalar(shift[:], root[:], 0.3 / math.sqrt(Z), 0.3 * 0.2, ALU.mult, ALU.add)
        log_denom = tile("log_denom", [P, 2], F32)
        nc.scalar.activation(log_denom[:], root[:], ACT.Ln, scale=1.0 / math.sqrt(Z), bias=0.2)

        for b in range(2):
            for h in range(2):
                cols = slice(HALF * h, HALF * (h + 1))
                logs = tile("logs%d_%d" % (b, h), [P, HALF], F32)
                nc.scalar.activation(logs[:], mu[b][:, cols], ACT.Ln, bias=shift[:, b : b + 1])
                result = tile("result%d_%d" % (b, h), [P, HALF], F32)
                nc.vector.scalar_tensor_tensor(result[:], logs[:], log_denom[:, b : b + 1], fee[:, cols], ALU.subtract, ALU.mult)
                nc.sync.dma_start(out[P * b : P * (b + 1), cols], result[:])
